import numpy as np
import ml_dtypes


def mxq(x, axis, fmt="e4m3"):
    dtype, down = {"e4m3": (ml_dtypes.float8_e4m3fn, 7), "e5m2": (ml_dtypes.float8_e5m2, 14)}[fmt]
    v = np.moveaxis(np.asarray(x, np.float32).astype(ml_dtypes.bfloat16).astype(np.float64), axis, -1)
    blocks = v.reshape(v.shape[:-1] + (-1, 32))
    amax = np.abs(blocks).max(-1, keepdims=True)
    byte = np.maximum(np.where(amax > 0, np.frexp(amax)[1] - 1 + 127, 0) - down, 1)
    scale = np.exp2(byte - 127.0)
    codes = (blocks / scale).astype(np.float32).astype(dtype).astype(np.float64)
    return np.moveaxis((codes * scale).reshape(v.shape), -1, axis)


WIDE = False


def mx_kscale(k):
    if not WIDE:
        return np.ones(k)
    levels = np.array([10, -10, 5, -5, 0])
    if k % 512:
        return np.exp2(np.random.permutation(np.resize(levels, k // 32))).repeat(32)
    a = np.empty((k // 512, 16))
    for p in range(k // 512):
        a[p, :8] = np.random.permutation(np.resize(levels, 8))
        for g in range(8):
            far = levels[np.abs(levels - a[p, g]) >= 10]
            a[p, g + 8] = far[np.random.randint(len(far))]
    return np.exp2(a.ravel()).repeat(32)


def f64(x):
    return np.asarray(x).astype(np.float64)


def striped(idx):
    return np.tile(np.asarray(idx).reshape(-1, 16).T, (8, 1)).astype(np.uint16)


def unstriped(offs):
    return offs[:16].T.reshape(-1).astype(np.int64)


E2M1 = np.array([0.0, 0.5, 1.0, 1.5, 2.0, 3.0, 4.0, 6.0, -0.0, -0.5, -1.0, -1.5, -2.0, -3.0, -4.0, -6.0])


def pack_weight(w, fmt):
    k, n = w.shape
    w = f64(np.asarray(w, np.float32).astype(ml_dtypes.bfloat16)).reshape(k // 32, 32, n)
    amax = np.abs(w).max(1)
    if fmt == "e4m3":
        byte = np.frexp(amax)[1] - 1 + 127 - 7
    else:
        mant, ex = np.frexp(amax / 6.0)
        byte = np.where(mant > 0.5, ex, ex - 1) + 127
    byte = np.clip(np.where(amax > 0, byte, 1), 1, 254)
    scaled = (w * np.exp2(127.0 - byte)[:, None, :]).reshape(k, n).astype(np.float32)
    by_word = np.ascontiguousarray(scaled.reshape(k // 512, 128, 4, n).transpose(0, 1, 3, 2))
    if fmt == "e4m3":
        words = by_word.astype(ml_dtypes.float8_e4m3fn).view(np.uint8)
    else:
        c = by_word.astype(ml_dtypes.float4_e2m1fn).view(np.uint8) & 0xF
        words = (c[..., 0::2] | (c[..., 1::2] << 4)).reshape(k // 512, 128, 2 * n)
    return np.ascontiguousarray(words), np.ascontiguousarray(byte.astype(np.uint8).reshape(k // 512, 16, n))


def unpack_weight(words, scales, fmt):
    g, _, n = scales.shape
    words = np.ascontiguousarray(words).reshape(g, 128, n, -1)
    if fmt == "e4m3":
        vals = words.view(ml_dtypes.float8_e4m3fn).astype(np.float64)
    else:
        nib = np.empty((g, 128, n, 4), np.uint8)
        nib[..., 0::2] = words & 0xF
        nib[..., 1::2] = words >> 4
        vals = E2M1[nib]
    vals = vals * np.repeat(np.exp2(scales.astype(np.float64) - 127.0), 8, axis=1)[..., None]
    return vals.transpose(0, 1, 3, 2).reshape(g * 512, n)


D, T, I, Q, E = 512, 2048, 512, 128, 512


def setup_inputs():
    n = np.random.standard_normal
    idx = np.random.permutation(T)[:I]
    fd = mx_kscale(D)
    fi = mx_kscale(I)
    ti = np.ones(T)
    ti[idx] = fi
    keysp = pack_weight(n((D, T)) / fd[:, None], "e4m3")
    return {
        "query": (n((D, Q)) * 0.6 / np.sqrt(D) * fd[:, None]).astype(np.float32),
        "keys_words": keysp[0],
        "keys_scales": keysp[1],
        "level": (np.random.uniform(0.5, 0.9, (Q, 1))).astype(np.float32),
        "size": (np.random.uniform(0.5, 2.0, (1, I)) * fi).astype(np.float32),
        "vals": (n((E, T)) / ti).astype(np.float32),
        "offs": striped(idx),
    }


def reference(query, keys_words, keys_scales, level, size, vals, offs):
    idx = unstriped(offs)
    keysu = unpack_weight(keys_words, keys_scales, "e4m3")
    queryq = mxq(f64(query), 0, "e4m3")
    keysidxg = keysu[:, idx]
    a = queryq.T @ keysidxg
    p = np.exp(a - np.max(a, axis=1, keepdims=True))
    r = np.maximum(p / np.sum(p, axis=1, keepdims=True) * 512.0 - f64(level), 0.0)
    w = r * f64(size) / np.sum(r, axis=1, keepdims=True)
    wt = w.T
    vt = f64(vals)[:, idx].T
    wtq = mxq(wt, 0, "e4m3")
    vtq = mxq(vt, 0, "e4m3")
    o = wtq.T @ vtq
    return o

@@ -1,0 +1,175 @@
+from contextlib import ExitStack
+
+import concourse.mybir as mybir
+from concourse.masks import make_identity
+
+D, T, I, Q, E = 512, 2048, 512, 128, 512
+FLOPS = 2 * Q * I * D + 2 * Q * E * I
+
+F32 = mybir.dt.float32
+BF16 = mybir.dt.bfloat16
+I32 = mybir.dt.int32
+U32 = mybir.dt.uint32
+U16 = mybir.dt.uint16
+U8 = mybir.dt.uint8
+FP8X4 = mybir.dt.float8_e4m3fn_x4
+ACT = mybir.ActivationFunctionType
+ALU = mybir.AluOpType
+AXIS = mybir.AxisListType
+
+P = 128
+PACK = 4
+BLOCKS = E // P
+
+
+def tile_attend_sharesabove_kernel(tc, query, keys_words, keys_scales, level, size, vals, offs, out):
+    nc = tc.nc
+    with ExitStack() as ctx:
+        keep = ctx.enter_context(tc.tile_pool(name="keep", bufs=1))
+        psum = ctx.enter_context(tc.psum_pool(name="psum", bufs=1))
+
+        offsets = keep.tile([P, I // 16], U16, name="offsets")
+        q_raw = keep.tile([P, PACK, Q], F32, name="q_raw")
+        key_pool = keep.tile([P, T], I32, name="key_pool")
+        scale_pool = keep.tile([P, T], U8, name="scale_pool", tag="scale_pool")
+        val_pool = [keep.tile([P, T], F32, name="val_pool%d" % b, tag="val_pool%d" % b, align_bytes=64) for b in range(BLOCKS)]
+        level_col = keep.tile([P, 1], F32, name="level_col")
+        size_cols = keep.tile([P, PACK], F32, name="size_cols")
+        ident = keep.tile([P, P], F32, name="ident")
+
+        nc.vector.memset(scale_pool[:].bitcast(I32), 0)
+        nc.sync.dma_start(offsets[:], offs)
+        nc.sync.dma_start(q_raw[:], query.rearrange("(p j) q -> p j q", j=PACK))
+        nc.sync.dma_start(key_pool[:], keys_words[0].rearrange("p n t -> p (n t)").bitcast(I32))
+        for quad in range(4):
+            nc.scalar.dma_start(
+                scale_pool[32 * quad : 32 * quad + 4, :].bitcast(I32),
+                keys_scales[0, 4 * quad : 4 * quad + 4, :].bitcast(I32),
+            )
+        for b in range(BLOCKS):
+            nc.sync.dma_start(val_pool[b][:], vals[b * P : (b + 1) * P, :])
+        nc.gpsimd.dma_start(level_col[:], level)
+        nc.gpsimd.dma_start(size_cols[:], size.rearrange("o (p j) -> (o p) j", j=PACK))
+        make_identity(nc, ident[:])
+
+        def turn_and_quantize(src, name, bank_tag):
+            words = src[:].bitcast(F32)
+            turned = psum.tile([P, 2, P], F32, name=name + "_turned", tag=bank_tag)
+            for u in range(2):
+                nc.tensor.transpose(turned[:, u, :], words[:, u : 2 * P : 2], ident[:])
+            grouped = keep.tile([P, PACK * P], BF16, name=name + "_grouped", align_bytes=64)
+            nc.scalar.copy(
+                grouped[:].bitcast(F32).rearrange("p (c u) -> p c u", u=2),
+                turned[:].rearrange("p u c -> p c u"),
+            )
+            return grouped
+
+        def quantize(grouped, name, tag):
+            codes = keep.tile([P, P], U32, name=name + "_codes", tag=tag, align_bytes=64)
+            scales = keep.tile([P, P], U8, name=name + "_scales", align_bytes=64)
+            nc.vector.quantize_mx(out=codes[:].bitcast(FP8X4), scales=scales[:], in_=grouped[:])
+            return codes, scales
+
+        def gather_vals(b):
+            picked = keep.tile([P, I], BF16, name="picked%d" % b, tag="scale_pool" if b == 0 else "picked%d" % b)
+            nc.vector.tensor_copy(picked[:], val_pool[b][:].indirect(offsets[:]))
+            return picked
+
+        def turn_vals(picked, b):
+            return turn_and_quantize(picked, "v%d" % b, "turn%d" % (b % 2))
+
+        neg_level = keep.tile([P, 1], F32, name="neg_level")
+        nc.gpsimd.tensor_scalar(neg_level[:], level_col[:], -1.0 / I, 0.0, ALU.mult, ALU.add)
+        q_grouped = keep.tile([P, Q, PACK], BF16, name="q_grouped", align_bytes=64)
+        nc.scalar.copy(q_grouped[:], q_raw[:].rearrange("p j q -> p q j"))
+        key_scales = keep.tile([P, I], U8, name="key_scales", align_bytes=64)
+        nc.vector.tensor_copy(key_scales[:], scale_pool[:].indirect(offsets[:]))
+        q_codes = keep.tile([P, Q], U32, name="q_codes", align_bytes=64)
+        q_scales = keep.tile([P, Q], U8, name="q_scales", align_bytes=64)
+        nc.vector.quantize_mx(
+            out=q_codes[:].bitcast(FP8X4), scales=q_scales[:], in_=q_grouped[:].rearrange("p q j -> p (q j)")
+        )
+        key_codes = keep.tile([P, I], U32, name="key_codes", align_bytes=64)
+        nc.vector.tensor_copy(key_codes[:], key_pool[:].bitcast(U32).indirect(offsets[:]))
+
+        scores = psum.tile([P, I], F32, name="scores")
+        nc.tensor.matmul_mx(
+            out=scores[:],
+            lhsT=q_codes[:].bitcast(FP8X4),
+            lhsT_scale=q_scales[:],
+            rhs=key_codes[:].bitcast(FP8X4),
+            rhs_scale=key_scales[:],
+            start=True,
+            stop=True,
+        )
+        size_rows = psum.tile([P, PACK, P], F32, name="size_rows")
+        for j in range(PACK):
+            nc.tensor.transpose(size_rows[:, j, :], size_cols[:, j : j + 1].to_broadcast([P, P]), ident[:])
+
+        neg_max = keep.tile([P, 1], F32, name="neg_max")
+        nc.vector.tensor_reduce(neg_max[:], scores[:], AXIS.X, ALU.max, negate=True)
+        picked0 = gather_vals(0)
+
+        probs = keep.tile([P, I], F32, name="probs")
+        prob_sum = keep.tile([P, 1], F32, name="prob_sum")
+        nc.scalar.activation(probs[:], scores[:], ACT.Exp, bias=neg_max[:], accum_out=prob_sum[:])
+        neg_bar = keep.tile([P, 1], F32, name="neg_bar")
+        nc.scalar.activation(neg_bar[:], prob_sum[:], ACT.Copy, scale=neg_level[:])
+        above = keep.tile([P, I], F32, name="above")
+        above_sum = keep.tile([P, 1], F32, name="above_sum")
+        nc.scalar.activation(above[:], probs[:], ACT.Relu, bias=neg_bar[:], accum_out=above_sum[:])
+        v_grouped = [turn_vals(picked0, 0)]
+        inv_sum = keep.tile([P, 1], F32, name="inv_sum")
+        nc.vector.reciprocal(inv_sum[:], above_sum[:])
+        weights = keep.tile([P, I], BF16, name="weights")
+        nc.vector.scalar_tensor_tensor(
+            weights[:].rearrange("p (s j) -> p s j", j=PACK),
+            above[:].rearrange("p (s j) -> p s j", j=PACK),
+            inv_sum[:],
+            size_rows[:].rearrange("p j s -> p s j"),
+            ALU.mult,
+            ALU.mult,
+        )
+        w_grouped = turn_and_quantize(weights, "w", "turn_w")
+
+        picked1 = gather_vals(1)
+        v_quant = [quantize(v_grouped[0], "v0", "v0_codes")]
+        w_codes, w_scales = quantize(w_grouped, "w", "w_codes")
+        v_grouped.append(turn_vals(picked1, 1))
+
+        def product(dst, b):
+            codes, scales = v_quant[b]
+            nc.tensor.matmul_mx(
+                out=dst,
+                lhsT=w_codes[:].bitcast(FP8X4),
+                lhsT_scale=w_scales[:],
+                rhs=codes[:].bitcast(FP8X4),
+                rhs_scale=scales[:],
+                start=True,
+                stop=True,
+            )
+
+        head = psum.tile([P, 2 * P], F32, name="head")
+        product(head[:, 0:P], 0)
+        picked2 = gather_vals(2)
+        v_quant.append(quantize(v_grouped[1], "v1", "v1_codes"))
+        v_grouped.append(turn_vals(picked2, 2))
+        product(head[:, P : 2 * P], 1)
+        head_out = keep.tile([P, 2 * P], F32, name="head_out")
+        nc.scalar.copy(head_out[:], head[:])
+        nc.sync.dma_start(out[:, 0 : 2 * P], head_out[:])
+
+        picked3 = gather_vals(3)
+        v_grouped.append(turn_vals(picked3, 3))
+        v_quant.append(quantize(v_grouped[2], "v2", "val_pool3"))
+        third = psum.tile([P, P], F32, name="third")
+        product(third[:], 2)
+        third_out = keep.tile([P, P], F32, name="third_out")
+        nc.scalar.copy(third_out[:], third[:])
+        nc.sync.dma_start(out[:, 2 * P : 3 * P], third_out[:])
+        v_quant.append(quantize(v_grouped[3], "v3", "v3_codes"))
+        last = psum.tile([P, P], F32, name="last")
+        product(last[:], 3)
+        last_out = keep.tile([P, P], F32, name="last_out")
+        nc.vector.tensor_copy(last_out[:], last[:])
+        nc.sync.dma_start(out[:, 3 * P : E], last_out[:])

@@ -31,7 +31,7 @@ def tile_attend_sharesabove_kernel(tc, query, keys_words, keys_scales, level, si
         offsets = keep.tile([P, I // 16], U16, name="offsets")
         q_raw = keep.tile([P, PACK, Q], F32, name="q_raw")
         key_pool = keep.tile([P, T], I32, name="key_pool")
-        scale_pool = keep.tile([P, T], U8, name="scale_pool", tag="scale_pool")
+        scale_pool = keep.tile([P, T], U8, name="scale_pool")
         val_pool = [keep.tile([P, T], F32, name="val_pool%d" % b, tag="val_pool%d" % b, align_bytes=64) for b in range(BLOCKS)]
         level_col = keep.tile([P, 1], F32, name="level_col")
         size_cols = keep.tile([P, PACK], F32, name="size_cols")
@@ -40,43 +40,36 @@ def tile_attend_sharesabove_kernel(tc, query, keys_words, keys_scales, level, si
         nc.vector.memset(scale_pool[:].bitcast(I32), 0)
         nc.sync.dma_start(offsets[:], offs)
         nc.sync.dma_start(q_raw[:], query.rearrange("(p j) q -> p j q", j=PACK))
-        nc.sync.dma_start(key_pool[:], keys_words[0].rearrange("p n t -> p (n t)").bitcast(I32))
         for quad in range(4):
-            nc.scalar.dma_start(
+            (nc.sync if quad < 2 else nc.scalar).dma_start(
                 scale_pool[32 * quad : 32 * quad + 4, :].bitcast(I32),
                 keys_scales[0, 4 * quad : 4 * quad + 4, :].bitcast(I32),
             )
+        nc.sync.dma_start(key_pool[:], keys_words[0].rearrange("p n t -> p (n t)").bitcast(I32))
+        nc.sync.dma_start(level_col[:], level)
         for b in range(BLOCKS):
             nc.sync.dma_start(val_pool[b][:], vals[b * P : (b + 1) * P, :])
-        nc.gpsimd.dma_start(level_col[:], level)
-        nc.gpsimd.dma_start(size_cols[:], size.rearrange("o (p j) -> (o p) j", j=PACK))
+            if b == 0:
+                nc.sync.dma_start(size_cols[:], size.rearrange("o (p j) -> (o p) j", j=PACK))
         make_identity(nc, ident[:])
 
-        def turn_and_quantize(src, name, bank_tag):
+        def turn(src, grouped, name, bank_tag):
             words = src[:].bitcast(F32)
-            turned = psum.tile([P, 2, P], F32, name=name + "_turned", tag=bank_tag)
+            turned = psum.tile([P, 2, P], F32, name=name, tag=bank_tag)
             for u in range(2):
                 nc.tensor.transpose(turned[:, u, :], words[:, u : 2 * P : 2], ident[:])
-            grouped = keep.tile([P, PACK * P], BF16, name=name + "_grouped", align_bytes=64)
             nc.scalar.copy(
-                grouped[:].bitcast(F32).rearrange("p (c u) -> p c u", u=2),
+                grouped.bitcast(F32).rearrange("p (c u) -> p c u", u=2),
                 turned[:].rearrange("p u c -> p c u"),
             )
-            return grouped
-
-        def quantize(grouped, name, tag):
-            codes = keep.tile([P, P], U32, name=name + "_codes", tag=tag, align_bytes=64)
-            scales = keep.tile([P, P], U8, name=name + "_scales", align_bytes=64)
-            nc.vector.quantize_mx(out=codes[:].bitcast(FP8X4), scales=scales[:], in_=grouped[:])
-            return codes, scales
 
         def gather_vals(b):
-            picked = keep.tile([P, I], BF16, name="picked%d" % b, tag="scale_pool" if b == 0 else "picked%d" % b)
+            picked = keep.tile([P, I], BF16, name="picked%d" % b)
             nc.vector.tensor_copy(picked[:], val_pool[b][:].indirect(offsets[:]))
             return picked
 
-        def turn_vals(picked, b):
-            return turn_and_quantize(picked, "v%d" % b, "turn%d" % (b % 2))
+        def quantize(codes, scales, grouped):
+            nc.vector.quantize_mx(out=codes.bitcast(FP8X4), scales=scales, in_=grouped)
 
         neg_level = keep.tile([P, 1], F32, name="neg_level")
         nc.gpsimd.tensor_scalar(neg_level[:], level_col[:], -1.0 / I, 0.0, ALU.mult, ALU.add)
@@ -118,8 +111,11 @@ def tile_attend_sharesabove_kernel(tc, query, keys_words, keys_scales, level, si
         above = keep.tile([P, I], F32, name="above")
         above_sum = keep.tile([P, 1], F32, name="above_sum")
         nc.scalar.activation(above[:], probs[:], ACT.Relu, bias=neg_bar[:], accum_out=above_sum[:])
-        v_grouped = [turn_vals(picked0, 0)]
-        inv_sum = keep.tile([P, 1], F32, name="inv_sum")
+        v01_grouped = keep.tile([P, 2 * I], BF16, name="v01_grouped", align_bytes=64)
+        turn(picked0, v01_grouped[:, 0:I], "v0_turned", "turn0")
+        picked1 = gather_vals(1)
+        turn(picked1, v01_grouped[:, I : 2 * I], "v1_turned", "turn1")
+        inv_sum = keep.tile([P, 1], F32, name="inv_sum", tag="val_pool1", align_bytes=64)
         nc.vector.reciprocal(inv_sum[:], above_sum[:])
         weights = keep.tile([P, I], BF16, name="weights")
         nc.vector.scalar_tensor_tensor(
@@ -130,46 +126,45 @@ def tile_attend_sharesabove_kernel(tc, query, keys_words, keys_scales, level, si
             ALU.mult,
             ALU.mult,
         )
-        w_grouped = turn_and_quantize(weights, "w", "turn_w")
+        w_grouped = keep.tile([P, I], BF16, name="w_grouped", align_bytes=64)
+        turn(weights, w_grouped[:], "w_turned", "turn_w")
 
-        picked1 = gather_vals(1)
-        v_quant = [quantize(v_grouped[0], "v0", "v0_codes")]
-        w_codes, w_scales = quantize(w_grouped, "w", "w_codes")
-        v_grouped.append(turn_vals(picked1, 1))
+        picked2 = gather_vals(2)
+        v2_grouped = keep.tile([P, I], BF16, name="v2_grouped", align_bytes=64)
+        turn(picked2, v2_grouped[:], "v2_turned", "turn0")
+        early_codes = keep.tile([P, 3 * P], U32, name="early_codes", tag="val_pool2", align_bytes=64)
+        v01_scales = keep.tile([P, 2 * P], U8, name="v01_scales", align_bytes=64)
+        w_scales = keep.tile([P, P], U8, name="w_scales", align_bytes=64)
+        v01_codes = early_codes[:, 0 : 2 * P]
+        w_codes = early_codes[:, 2 * P : 3 * P]
+        quantize(v01_codes, v01_scales[:], v01_grouped[:])
+        quantize(w_codes, w_scales[:], w_grouped[:])
 
-        def product(dst, b):
-            codes, scales = v_quant[b]
+        def product(codes, scales, first, width, copy):
+            bank = psum.tile([P, width], F32, name="product%d" % first)
             nc.tensor.matmul_mx(
-                out=dst,
-                lhsT=w_codes[:].bitcast(FP8X4),
+                out=bank[:],
+                lhsT=w_codes.bitcast(FP8X4),
                 lhsT_scale=w_scales[:],
-                rhs=codes[:].bitcast(FP8X4),
-                rhs_scale=scales[:],
+                rhs=codes.bitcast(FP8X4),
+                rhs_scale=scales,
                 start=True,
                 stop=True,
             )
+            result = keep.tile([P, width], F32, name="result%d" % first)
+            copy(result[:], bank[:])
+            nc.sync.dma_start(out[:, first : first + width], result[:])
 
-        head = psum.tile([P, 2 * P], F32, name="head")
-        product(head[:, 0:P], 0)
-        picked2 = gather_vals(2)
-        v_quant.append(quantize(v_grouped[1], "v1", "v1_codes"))
-        v_grouped.append(turn_vals(picked2, 2))
-        product(head[:, P : 2 * P], 1)
-        head_out = keep.tile([P, 2 * P], F32, name="head_out")
-        nc.scalar.copy(head_out[:], head[:])
-        nc.sync.dma_start(out[:, 0 : 2 * P], head_out[:])
+        product(v01_codes, v01_scales[:], 0, 2 * P, nc.scalar.copy)
 
         picked3 = gather_vals(3)
-        v_grouped.append(turn_vals(picked3, 3))
-        v_quant.append(quantize(v_grouped[2], "v2", "val_pool3"))
-        third = psum.tile([P, P], F32, name="third")
-        product(third[:], 2)
-        third_out = keep.tile([P, P], F32, name="third_out")
-        nc.scalar.copy(third_out[:], third[:])
-        nc.sync.dma_start(out[:, 2 * P : 3 * P], third_out[:])
-        v_quant.append(quantize(v_grouped[3], "v3", "v3_codes"))
-        last = psum.tile([P, P], F32, name="last")
-        product(last[:], 3)
-        last_out = keep.tile([P, P], F32, name="last_out")
-        nc.vector.tensor_copy(last_out[:], last[:])
-        nc.sync.dma_start(out[:, 3 * P : E], last_out[:])
+        v3_grouped = keep.tile([P, I], BF16, name="v3_grouped", align_bytes=64)
+        turn(picked3, v3_grouped[:], "v3_turned", "turn1")
+        v2_codes = keep.tile([P, P], U32, name="v2_codes", tag="val_pool3", align_bytes=64)
+        v2_scales = keep.tile([P, P], U8, name="v2_scales", align_bytes=64)
+        quantize(v2_codes[:], v2_scales[:], v2_grouped[:])
+        product(v2_codes[:], v2_scales[:], 2 * P, P, nc.scalar.copy)
+        v3_codes = keep.tile([P, P], U32, name="v3_codes", align_bytes=64)
+        v3_scales = keep.tile([P, P], U8, name="v3_scales", align_bytes=64)
+        quantize(v3_codes[:], v3_scales[:], v3_grouped[:])
+        product(v3_codes[:], v3_scales[:], 3 * P, P, nc.vector.tensor_copy)

from contextlib import ExitStack

import concourse.mybir as mybir
from concourse.masks import make_identity

D, T, I, Q, E = 512, 2048, 512, 128, 512
FLOPS = 2 * Q * I * D + 2 * Q * E * I

F32 = mybir.dt.float32
BF16 = mybir.dt.bfloat16
I32 = mybir.dt.int32
U32 = mybir.dt.uint32
U16 = mybir.dt.uint16
U8 = mybir.dt.uint8
FP8X4 = mybir.dt.float8_e4m3fn_x4
ACT = mybir.ActivationFunctionType
ALU = mybir.AluOpType
AXIS = mybir.AxisListType

P = 128
PACK = 4
BLOCKS = E // P


def tile_attend_sharesabove_kernel(tc, query, keys_words, keys_scales, level, size, vals, offs, out):
    nc = tc.nc
    with ExitStack() as ctx:
        keep = ctx.enter_context(tc.tile_pool(name="keep", bufs=1))
        psum = ctx.enter_context(tc.psum_pool(name="psum", bufs=1))

        offsets = keep.tile([P, I // 16], U16, name="offsets")
        q_raw = keep.tile([P, PACK, Q], F32, name="q_raw")
        key_pool = keep.tile([P, T], I32, name="key_pool")
        scale_pool = keep.tile([P, T], U8, name="scale_pool")
        val_pool = [keep.tile([P, T], F32, name="val_pool%d" % b, tag="val_pool%d" % b, align_bytes=64) for b in range(BLOCKS)]
        level_col = keep.tile([P, 1], F32, name="level_col")
        size_cols = keep.tile([P, PACK], F32, name="size_cols")
        ident = keep.tile([P, P], F32, name="ident")

        nc.vector.memset(scale_pool[:].bitcast(I32), 0)
        nc.sync.dma_start(offsets[:], offs)
        nc.sync.dma_start(q_raw[:], query.rearrange("(p j) q -> p j q", j=PACK))
        for quad in range(4):
            (nc.sync if quad < 2 else nc.scalar).dma_start(
                scale_pool[32 * quad : 32 * quad + 4, :].bitcast(I32),
                keys_scales[0, 4 * quad : 4 * quad + 4, :].bitcast(I32),
            )
        nc.sync.dma_start(key_pool[:], keys_words[0].rearrange("p n t -> p (n t)").bitcast(I32))
        nc.sync.dma_start(level_col[:], level)
        for b in range(BLOCKS):
            nc.sync.dma_start(val_pool[b][:], vals[b * P : (b + 1) * P, :])
            if b == 0:
                nc.sync.dma_start(size_cols[:], size.rearrange("o (p j) -> (o p) j", j=PACK))
        make_identity(nc, ident[:])

        def turn(src, grouped, name, bank_tag):
            words = src[:].bitcast(F32)
            turned = psum.tile([P, 2, P], F32, name=name, tag=bank_tag)
            for u in range(2):
                nc.tensor.transpose(turned[:, u, :], words[:, u : 2 * P : 2], ident[:])
            nc.scalar.copy(
                grouped.bitcast(F32).rearrange("p (c u) -> p c u", u=2),
                turned[:].rearrange("p u c -> p c u"),
            )

        def gather_vals(b):
            picked = keep.tile([P, I], BF16, name="picked%d" % b)
            nc.vector.tensor_copy(picked[:], val_pool[b][:].indirect(offsets[:]))
            return picked

        def quantize(codes, scales, grouped):
            nc.vector.quantize_mx(out=codes.bitcast(FP8X4), scales=scales, in_=grouped)

        neg_level = keep.tile([P, 1], F32, name="neg_level")
        nc.gpsimd.tensor_scalar(neg_level[:], level_col[:], -1.0 / I, 0.0, ALU.mult, ALU.add)
        q_grouped = keep.tile([P, Q, PACK], BF16, name="q_grouped", align_bytes=64)
        nc.scalar.copy(q_grouped[:], q_raw[:].rearrange("p j q -> p q j"))
        key_scales = keep.tile([P, I], U8, name="key_scales", align_bytes=64)
        nc.vector.tensor_copy(key_scales[:], scale_pool[:].indirect(offsets[:]))
        q_codes = keep.tile([P, Q], U32, name="q_codes", align_bytes=64)
        q_scales = keep.tile([P, Q], U8, name="q_scales", align_bytes=64)
        nc.vector.quantize_mx(
            out=q_codes[:].bitcast(FP8X4), scales=q_scales[:], in_=q_grouped[:].rearrange("p q j -> p (q j)")
        )
        key_codes = keep.tile([P, I], U32, name="key_codes", align_bytes=64)
        nc.vector.tensor_copy(key_codes[:], key_pool[:].bitcast(U32).indirect(offsets[:]))

        scores = psum.tile([P, I], F32, name="scores")
        nc.tensor.matmul_mx(
            out=scores[:],
            lhsT=q_codes[:].bitcast(FP8X4),
            lhsT_scale=q_scales[:],
            rhs=key_codes[:].bitcast(FP8X4),
            rhs_scale=key_scales[:],
            start=True,
            stop=True,
        )
        size_rows = psum.tile([P, PACK, P], F32, name="size_rows")
        for j in range(PACK):
            nc.tensor.transpose(size_rows[:, j, :], size_cols[:, j : j + 1].to_broadcast([P, P]), ident[:])

        neg_max = keep.tile([P, 1], F32, name="neg_max")
        nc.vector.tensor_reduce(neg_max[:], scores[:], AXIS.X, ALU.max, negate=True)
        picked0 = gather_vals(0)

        probs = keep.tile([P, I], F32, name="probs")
        prob_sum = keep.tile([P, 1], F32, name="prob_sum")
        nc.scalar.activation(probs[:], scores[:], ACT.Exp, bias=neg_max[:], accum_out=prob_sum[:])
        neg_bar = keep.tile([P, 1], F32, name="neg_bar")
        nc.scalar.activation(neg_bar[:], prob_sum[:], ACT.Copy, scale=neg_level[:])
        above = keep.tile([P, I], F32, name="above")
        above_sum = keep.tile([P, 1], F32, name="above_sum")
        nc.scalar.activation(above[:], probs[:], ACT.Relu, bias=neg_bar[:], accum_out=above_sum[:])
        v01_grouped = keep.tile([P, 2 * I], BF16, name="v01_grouped", align_bytes=64)
        turn(picked0, v01_grouped[:, 0:I], "v0_turned", "turn0")
        picked1 = gather_vals(1)
        turn(picked1, v01_grouped[:, I : 2 * I], "v1_turned", "turn1")
        inv_sum = keep.tile([P, 1], F32, name="inv_sum", tag="val_pool1", align_bytes=64)
        nc.vector.reciprocal(inv_sum[:], above_sum[:])
        weights = keep.tile([P, I], BF16, name="weights")
        nc.vector.scalar_tensor_tensor(
            weights[:].rearrange("p (s j) -> p s j", j=PACK),
            above[:].rearrange("p (s j) -> p s j", j=PACK),
            inv_sum[:],
            size_rows[:].rearrange("p j s -> p s j"),
            ALU.mult,
            ALU.mult,
        )
        w_grouped = keep.tile([P, I], BF16, name="w_grouped", align_bytes=64)
        turn(weights, w_grouped[:], "w_turned", "turn_w")

        picked2 = gather_vals(2)
        v2_grouped = keep.tile([P, I], BF16, name="v2_grouped", align_bytes=64)
        turn(picked2, v2_grouped[:], "v2_turned", "turn0")
        early_codes = keep.tile([P, 3 * P], U32, name="early_codes", tag="val_pool2", align_bytes=64)
        v01_scales = keep.tile([P, 2 * P], U8, name="v01_scales", align_bytes=64)
        w_scales = keep.tile([P, P], U8, name="w_scales", align_bytes=64)
        v01_codes = early_codes[:, 0 : 2 * P]
        w_codes = early_codes[:, 2 * P : 3 * P]
        quantize(v01_codes, v01_scales[:], v01_grouped[:])
        quantize(w_codes, w_scales[:], w_grouped[:])

        def product(codes, scales, first, width, copy):
            bank = psum.tile([P, width], F32, name="product%d" % first)
            nc.tensor.matmul_mx(
                out=bank[:],
                lhsT=w_codes.bitcast(FP8X4),
                lhsT_scale=w_scales[:],
                rhs=codes.bitcast(FP8X4),
                rhs_scale=scales,
                start=True,
                stop=True,
            )
            result = keep.tile([P, width], F32, name="result%d" % first)
            copy(result[:], bank[:])
            nc.sync.dma_start(out[:, first : first + width], result[:])

        product(v01_codes, v01_scales[:], 0, 2 * P, nc.scalar.copy)

        picked3 = gather_vals(3)
        v3_grouped = keep.tile([P, I], BF16, name="v3_grouped", align_bytes=64)
        turn(picked3, v3_grouped[:], "v3_turned", "turn1")
        v2_codes = keep.tile([P, P], U32, name="v2_codes", tag="val_pool3", align_bytes=64)
        v2_scales = keep.tile([P, P], U8, name="v2_scales", align_bytes=64)
        quantize(v2_codes[:], v2_scales[:], v2_grouped[:])
        product(v2_codes[:], v2_scales[:], 2 * P, P, nc.scalar.copy)
        v3_codes = keep.tile([P, P], U32, name="v3_codes", align_bytes=64)
        v3_scales = keep.tile([P, P], U8, name="v3_scales", align_bytes=64)
        quantize(v3_codes[:], v3_scales[:], v3_grouped[:])
        product(v3_codes[:], v3_scales[:], 3 * P, P, nc.vector.tensor_copy)
